import numpy as np
import ml_dtypes


def mxq(x, axis, fmt="e4m3"):
    dtype, down = {"e4m3": (ml_dtypes.float8_e4m3fn, 7), "e5m2": (ml_dtypes.float8_e5m2, 14)}[fmt]
    v = np.moveaxis(np.asarray(x, np.float32).astype(ml_dtypes.bfloat16).astype(np.float64), axis, -1)
    blocks = v.reshape(v.shape[:-1] + (-1, 32))
    amax = np.abs(blocks).max(-1, keepdims=True)
    byte = np.maximum(np.where(amax > 0, np.frexp(amax)[1] - 1 + 127, 0) - down, 1)
    scale = np.exp2(byte - 127.0)
    codes = (blocks / scale).astype(np.float32).astype(dtype).astype(np.float64)
    return np.moveaxis((codes * scale).reshape(v.shape), -1, axis)


WIDE = False


def mx_kscale(k):
    if not WIDE:
        return np.ones(k)
    levels = np.array([10, -10, 5, -5, 0])
    if k % 512:
        return np.exp2(np.random.permutation(np.resize(levels, k // 32))).repeat(32)
    a = np.empty((k // 512, 16))
    for p in range(k // 512):
        a[p, :8] = np.random.permutation(np.resize(levels, 8))
        for g in range(8):
            far = levels[np.abs(levels - a[p, g]) >= 10]
            a[p, g + 8] = far[np.random.randint(len(far))]
    return np.exp2(a.ravel()).repeat(32)


BF16 = ml_dtypes.bfloat16


def bf(x):
    return np.asarray(x, np.float32).astype(BF16)


def f64(x):
    return np.asarray(x).astype(np.float64)


E2M1 = np.array([0.0, 0.5, 1.0, 1.5, 2.0, 3.0, 4.0, 6.0, -0.0, -0.5, -1.0, -1.5, -2.0, -3.0, -4.0, -6.0])


def pack_weight(w, fmt):
    k, n = w.shape
    w = f64(bf(w)).reshape(k // 32, 32, n)
    amax = np.abs(w).max(1)
    if fmt == "e4m3":
        byte = np.frexp(amax)[1] - 1 + 127 - 7
    else:
        mant, ex = np.frexp(amax / 6.0)
        byte = np.where(mant > 0.5, ex, ex - 1) + 127
    byte = np.clip(np.where(amax > 0, byte, 1), 1, 254)
    scaled = (w * np.exp2(127.0 - byte)[:, None, :]).reshape(k, n).astype(np.float32)
    by_word = np.ascontiguousarray(scaled.reshape(k // 512, 128, 4, n).transpose(0, 1, 3, 2))
    if fmt == "e4m3":
        words = by_word.astype(ml_dtypes.float8_e4m3fn).view(np.uint8)
    else:
        c = by_word.astype(ml_dtypes.float4_e2m1fn).view(np.uint8) & 0xF
        words = c[..., 0::2] | (c[..., 1::2] << 4)
    return np.ascontiguousarray(words), np.ascontiguousarray(byte.astype(np.uint8).reshape(k // 512, 16, n))


def unpack_weight(words, scales, fmt):
    g, p, n, _ = words.shape
    if fmt == "e4m3":
        vals = np.ascontiguousarray(words).view(ml_dtypes.float8_e4m3fn).astype(np.float64)
    else:
        nib = np.empty((g, p, n, 4), np.uint8)
        nib[..., 0::2] = words & 0xF
        nib[..., 1::2] = words >> 4
        vals = E2M1[nib]
    vals = vals * np.repeat(np.exp2(scales.astype(np.float64) - 127.0), 8, axis=1)[..., None]
    return vals.transpose(0, 1, 3, 2).reshape(g * 512, n)
def pack4(w):
    words, scales = pack_weight(w, "e2m1")
    return words.reshape(words.shape[0], 128, -1), scales


def unpack4(words, scales):
    return unpack_weight(words.reshape(words.shape[0], 128, -1, 2), scales, "e2m1")


M, K, F, C, R = 1024, 1024, 1536, 1024, 512


def draw0():
    s, t, u = mx_kscale(K), mx_kscale(F), mx_kscale(M)
    x = np.random.standard_normal((M, K)) * s
    enc = np.random.standard_normal((K, F)) / np.sqrt(K) / s[:, None] * t
    bias = 0.3 * np.random.standard_normal(F) * t
    amp = (1 + 0.1 * np.random.standard_normal(M)) * u
    d_words, d_scales = pack4(np.random.standard_normal((F, C)) / np.sqrt(F) / t[:, None])
    attr = np.random.standard_normal((M, R)) / np.sqrt(M) / u[:, None]
    return {"x": bf(x), "enc": bf(enc), "bias": bf(bias), "amp": bf(amp),
            "d_words": d_words, "d_scales": d_scales, "attr": bf(attr)}


def core(x, enc, bias, amp, d_words, d_scales, attr):
    pre = mxq(f64(x), 1, "e4m3") @ mxq(f64(enc), 0, "e4m3")
    h = np.maximum(pre + f64(bias), 0.0) * f64(amp)[:, None]
    y = mxq(h, 1, "e4m3") @ unpack4(d_words, d_scales)
    z = mxq(h, 0, "e4m3").T @ mxq(f64(attr), 0, "e4m3")
    return y, z


def e4m3fn_bytes(y):
    return np.clip(np.asarray(y, np.float64), -448.0, 448.0).astype(np.float32).astype(ml_dtypes.float8_e4m3fn).view(np.uint8)


def e4m3fn_values(b):
    return np.asarray(b, np.uint8).view(ml_dtypes.float8_e4m3fn).astype(np.float64)


def setup_inputs():
    d = draw0()
    x0 = np.asarray(d['x']).astype(np.float64)
    s = (np.max(np.abs(x0), axis=(0,), keepdims=True) / 448.0).astype(np.float32)
    out = {}
    for k, v in d.items():
        if k == 'x':
            out['x_bytes'] = e4m3fn_bytes(x0 / s.astype(np.float64))
            out['x_scale'] = s
        else:
            out[k] = v
    return out


def reference(x_bytes, x_scale, enc, bias, amp, d_words, d_scales, attr):
    return core(e4m3fn_values(x_bytes) * x_scale.astype(np.float64), enc, bias, amp, d_words, d_scales, attr)

@@ -1,0 +1,440 @@
+from contextlib import ExitStack
+
+import concourse.mybir as mybir
+from concourse.masks import make_identity
+
+M, K, F, C, R = 1024, 1024, 1536, 1024, 512
+FLOPS = 2 * M * K * F + 2 * M * F * C + 2 * F * M * R
+
+F32 = mybir.dt.float32
+BF16 = mybir.dt.bfloat16
+U32 = mybir.dt.uint32
+I32 = mybir.dt.int32
+U8 = mybir.dt.uint8
+FP8 = mybir.dt.float8_e4m3fn
+FP8X4 = mybir.dt.float8_e4m3fn_x4
+FP4X4 = mybir.dt.float4_e2m1fn_x4
+ALU = mybir.AluOpType
+ACT = mybir.ActivationFunctionType
+
+P = 128
+KP = 512
+XP = K // KP
+FC = F // KP
+MH = M // KP
+
+
+def tile_relu_dictionary_readout_s8_kernel(tc, x_bytes, x_scale, enc, bias, amp, d_words, d_scales, attr, out_0, out_1):
+    nc = tc.nc
+    with ExitStack() as ctx:
+        keep = ctx.enter_context(tc.tile_pool(name="keep", bufs=1))
+        work = ctx.enter_context(tc.tile_pool(name="work", bufs=2))
+        psum = ctx.enter_context(tc.psum_pool(name="psum", bufs=1))
+
+        def kept(shape, dtype, name):
+            return keep.tile(shape, dtype, name=name, align_bytes=64)
+
+        def cols(count, name):
+            return kept([P, count], U32, "%s_codes" % name), kept([P, count], U8, "%s_scales" % name)
+
+        scale_sb = kept([P, K], F32, "scale_sb")
+        x_sb = [kept([P, 4, K], U8, "x_sb%d" % h) for h in range(MH)]
+        enc_sb = [[kept([P, 4, KP], BF16, "enc_sb%d%d" % (g, c)) for c in range(FC)] for g in range(XP)]
+        bias_sb = kept([P, FC, 4], BF16, "bias_sb")
+        amp_zs = kept([P, MH, 4], BF16, "amp_zs")
+        amp_sb = kept([P, M], BF16, "amp_sb")
+        d_sb = kept([P, FC, 2 * C], U8, "d_sb")
+        ds_sb = kept([P, FC, C], U8, "ds_sb")
+        attr_sb = [kept([P, 4, R], BF16, "attr_sb%d" % h) for h in range(MH)]
+
+        xv = x_bytes.rearrange("(h s p e) k -> h e p s k", h=MH, s=2, e=2)
+        ev = enc.rearrange("(g p j) f -> g p j f", p=P, j=4)
+        av = attr.rearrange("(h p u) r -> h p u r", p=P, u=4)
+
+        def load_enc(g, c):
+            nc.sync.dma_start(out=enc_sb[g][c][:], in_=ev[g][:, :, c * KP : (c + 1) * KP])
+
+        nc.gpsimd.memset(ds_sb[:].rearrange("p g n -> p (g n)").bitcast(I32), 0)
+        nc.sync.dma_start(out=scale_sb[:], in_=x_scale.rearrange("o k -> (o k)").partition_broadcast(P))
+        nc.sync.dma_start(out=x_sb[0][:, 0:2, :], in_=xv[0][0])
+        load_enc(0, 0)
+        nc.sync.dma_start(out=x_sb[0][:, 2:4, :], in_=xv[0][1])
+        load_enc(1, 0)
+        nc.sync.dma_start(out=amp_sb[:], in_=amp.partition_broadcast(P))
+        nc.sync.dma_start(out=bias_sb[:], in_=bias.rearrange("(c p t) -> p c t", p=P, t=4))
+        load_enc(0, 1)
+        load_enc(1, 1)
+        for e in range(2):
+            nc.sync.dma_start(out=x_sb[1][:, 2 * e : 2 * e + 2, :], in_=xv[1][e])
+        load_enc(0, 2)
+        load_enc(1, 2)
+        nc.sync.dma_start(out=amp_zs[:], in_=amp.rearrange("(h p u) -> p h u", p=P, u=4))
+        nc.sync.dma_start(out=d_sb[:], in_=d_words.rearrange("g p n -> p g n"))
+        for q in range(4):
+            nc.sync.dma_start(
+                out=ds_sb[32 * q : 32 * q + 4, :, :].bitcast(I32),
+                in_=d_scales[:, 4 * q : 4 * q + 4, :].rearrange("g q n -> q g n").bitcast(I32),
+            )
+        for h in range(MH):
+            nc.sync.dma_start(out=attr_sb[h][:], in_=av[h])
+
+        ident = kept([P, P], F32, "ident")
+        make_identity(nc, ident[:])
+        ident_bf = kept([P, P], BF16, "ident_bf")
+        nc.gpsimd.tensor_copy(out=ident_bf[:], in_=ident[:])
+
+        x_q = [[cols(KP, "x%d%d" % (h, g)) for g in range(XP)] for h in range(MH)]
+        e_q = [[cols(KP, "e%d%d" % (g, c)) for c in range(FC)] for g in range(XP)]
+        a_q = [cols(R, "a%d" % h) for h in range(MH)]
+        y_q = [[cols(KP, "y%d%d" % (h, c)) for c in range(FC)] for h in range(MH)]
+        z_q = [[cols(KP, "z%d%d" % (h, c)) for c in range(FC)] for h in range(MH)]
+        amp_abs = kept([P, M], BF16, "amp_abs")
+        sgn_z = kept([P, MH, 4], F32, "sgn_z")
+        sgn_y = kept([P, M // P], F32, "sgn_y")
+
+        x_grp = [None] * MH
+        e_grp = {}
+        a_sgn = {}
+        a_grp = {}
+        h_raw = {}
+        h_relu = {}
+        y_grp = {}
+        z_grp = {}
+
+        def quantize(pair, grouped):
+            nc.vector.quantize_mx(out=pair[0][:].bitcast(FP8X4), scales=pair[1][:], in_=grouped[:].rearrange("p w j -> p (w j)"))
+
+        def copy(engine, out, in_):
+            if engine == "s":
+                nc.scalar.copy(out=out, in_=in_)
+            else:
+                nc.vector.tensor_copy(out=out, in_=in_)
+
+        xbf = {}
+
+        def x_product(i):
+            xbf[i] = work.tile([P, K], BF16, name="xbf", align_bytes=64, bufs=3)
+            nc.vector.tensor_tensor(out=xbf[i][:], in0=x_sb[i // 4][:, i % 4, :].bitcast(FP8), in1=scale_sb[:], op=ALU.mult)
+
+        xt = {}
+
+        def x_transpose(i):
+            words = xbf[i][:].bitcast(F32)
+            xt[i] = psum.tile([P, XP, 2, P], F32, name="tp", bufs=2)
+            for g in range(XP):
+                for u in range(2):
+                    nc.tensor.transpose(xt[i][:, g, u, :], words[:, 256 * g + u : 256 * (g + 1) : 2], ident[:])
+
+        def x_copy(i, engine):
+            h, r = divmod(i, 4)
+            if r == 0:
+                x_grp[h] = work.tile([P, XP, KP, 4], BF16, name="x_grp", align_bytes=64, bufs=1)
+            dst = x_grp[h][:].rearrange("p g r j -> p (g r j)").bitcast(F32).rearrange("p (g r u) -> p g r u", g=XP, u=2)
+            copy(engine, dst[:, :, P * r : P * (r + 1), :], xt[i][:].rearrange("p g u r -> p g r u"))
+
+        def x_quant(h, g):
+            quantize(x_q[h][g], x_grp[h][:, g, :, :])
+
+        def e_group(g, c, t0, t1, engine):
+            if t0 == 0:
+                e_grp[g, c] = work.tile([P, KP, 4], BF16, name="e_grp", align_bytes=64, bufs=3)
+            dst = e_grp[g, c][:].rearrange("p (t m) j -> p t m j", t=4)
+            src = enc_sb[g][c][:].rearrange("p j (m t) -> p t m j", t=4)
+            copy(engine, dst[:, t0:t1], src[:, t0:t1])
+
+        def e_quant(g, c):
+            quantize(e_q[g][c], e_grp[g, c])
+
+        def a_sign(h):
+            a_sgn[h] = work.tile([P, 4, R], BF16, name="a_sgn", align_bytes=64, bufs=2)
+            for u in range(4):
+                nc.vector.tensor_scalar_mul(a_sgn[h][:, u, :], attr_sb[h][:, u, :], sgn_z[:, h, u : u + 1])
+
+        def interleave(dst, src, w0, w1, engine):
+            copy(
+                engine,
+                dst[:, w0:w1, :].rearrange("p (c i) t -> p c t i", i=4),
+                src[:, :, w0:w1].rearrange("p t (c i) -> p c t i", i=4),
+            )
+
+        def a_group(h, w0, w1, engine):
+            if w0 == 0:
+                a_grp[h] = work.tile([P, R, 4], BF16, name="a_grp", align_bytes=64, bufs=1)
+            copy(
+                engine,
+                a_grp[h][:, w0:w1, :].rearrange("p r (u e) -> p r u e", u=2),
+                a_sgn[h][:, :, w0:w1].rearrange("p (e u) r -> p r u e", e=2),
+            )
+
+        def a_quant(h):
+            quantize(a_q[h], a_grp[h])
+
+        pre = {}
+
+        def s1_mm(h, c, t):
+            pre[h, c, t] = psum.tile([P, KP], F32, name="mm", bufs=6)
+            for g in range(XP):
+                nc.tensor.matmul_mx(
+                    out=pre[h, c, t][:],
+                    lhsT=e_q[g][c][0][:, P * t : P * (t + 1)].bitcast(FP8X4),
+                    lhsT_scale=e_q[g][c][1][:, P * t : P * (t + 1)],
+                    rhs=x_q[h][g][0][:].bitcast(FP8X4),
+                    rhs_scale=x_q[h][g][1][:],
+                    start=(g == 0),
+                    stop=(g == XP - 1),
+                )
+
+        def s1_out(h, c, t):
+            if t == 0:
+                h_raw[h, c] = work.tile([P, 4, KP], BF16, name="h_raw", align_bytes=64, bufs=3)
+            nc.vector.scalar_tensor_tensor(
+                out=h_raw[h, c][:, t, :],
+                in0=pre[h, c, t][:],
+                scalar=bias_sb[:, c, t : t + 1],
+                in1=amp_abs[:, KP * h : KP * (h + 1)],
+                op0=ALU.add,
+                op1=ALU.mult,
+            )
+
+        def relu(h, c):
+            h_relu[h, c] = work.tile([P, 4, KP], BF16, name="h_relu", align_bytes=64, bufs=3)
+            nc.vector.tensor_scalar_max(h_relu[h, c][:], h_raw[h, c][:], 0.0)
+
+        def y_group(h, c, w0, w1, engine):
+            if w0 == 0:
+                y_grp[h, c] = work.tile([P, KP, 4], BF16, name="y_grp", align_bytes=64, bufs=3)
+            interleave(y_grp[h, c], h_relu[h, c], w0, w1, engine)
+
+        def y_quant(h, c):
+            quantize(y_q[h][c], y_grp[h, c])
+
+        zt = {}
+
+        def z_transpose(h, c, half):
+            zt[h, c, half] = psum.tile([P, 2, 2, P], F32, name="tp", bufs=2)
+            for tt in range(2):
+                words = h_relu[h, c][:, 2 * half + tt, :].bitcast(F32)
+                for u in range(2):
+                    nc.tensor.transpose(zt[h, c, half][:, tt, u, :], words[:, P * u : P * (u + 1)], ident[:])
+
+        def z_copy(h, c, half, engine):
+            if half == 0:
+                z_grp[h, c] = work.tile([P, KP, 4], BF16, name="z_grp", align_bytes=64, bufs=3)
+            dst = z_grp[h, c][:].rearrange("p n j -> p (n j)").bitcast(F32).rearrange("p (t n u) -> p t n u", t=4, u=2)
+            copy(engine, dst[:, 2 * half : 2 * half + 2], zt[h, c, half][:].rearrange("p t u n -> p t n u"))
+
+        def z_quant(h, c):
+            quantize(z_q[h][c], z_grp[h, c])
+
+        y_acc = {}
+        y_sb = {}
+
+        def y_mm(i, n, passes):
+            h, r = divmod(i, 4)
+            if passes[0] == 0:
+                y_acc[i, n] = psum.tile([P, KP], F32, name="mm", bufs=6)
+            for c in passes:
+                nc.tensor.matmul_mx(
+                    out=y_acc[i, n][:],
+                    lhsT=y_q[h][c][0][:, P * r : P * (r + 1)].bitcast(FP8X4),
+                    lhsT_scale=y_q[h][c][1][:, P * r : P * (r + 1)],
+                    rhs=d_sb[:, c, 2 * KP * n : 2 * KP * (n + 1)].bitcast(FP4X4),
+                    rhs_scale=ds_sb[:, c, KP * n : KP * (n + 1)],
+                    start=(c == 0),
+                    stop=(c == FC - 1),
+                )
+
+        yv = out_0.rearrange("(h s p e) c -> h e s p c", h=MH, s=2, e=2)
+
+        def y_out(i, n, engine):
+            h, r = divmod(i, 4)
+            sb = work.tile([P, KP], F32, name="y_sb", bufs=6)
+            if engine == "s":
+                nc.scalar.activation(out=sb[:], in_=y_acc[i, n][:], func=ACT.Copy, scale=sgn_y[:, i : i + 1])
+            else:
+                nc.vector.tensor_scalar_mul(sb[:], y_acc[i, n][:], sgn_y[:, i : i + 1])
+            nc.sync.dma_start(out=yv[h][r // 2][r % 2][:, KP * n : KP * (n + 1)], in_=sb[:])
+
+        zv = out_1.rearrange("(c p t) r -> c t p r", p=P, t=4)
+        z_acc = {}
+
+        def z_mm(c, t):
+            z_acc[c, t] = psum.tile([P, R], F32, name="mm", bufs=6)
+            for h in range(MH):
+                nc.tensor.matmul_mx(
+                    out=z_acc[c, t][:],
+                    lhsT=z_q[h][c][0][:, P * t : P * (t + 1)].bitcast(FP8X4),
+                    lhsT_scale=z_q[h][c][1][:, P * t : P * (t + 1)],
+                    rhs=a_q[h][0][:].bitcast(FP8X4),
+                    rhs_scale=a_q[h][1][:],
+                    start=(h == 0),
+                    stop=(h == MH - 1),
+                )
+
+        def z_out(c, t, engine):
+            sb = work.tile([P, R], F32, name="z_sb", bufs=6)
+            copy(engine, sb[:], z_acc[c, t][:])
+            nc.sync.dma_start(out=zv[c][t], in_=sb[:])
+
+        def e_s(g, c, ts=range(4)):
+            for t in ts:
+                e_group(g, c, t, t + 1, "s")
+
+        def e_v(g, c):
+            e_group(g, c, 0, 2, "v")
+            e_group(g, c, 2, 4, "v")
+
+        def xpre(i):
+            x_product(i)
+            x_transpose(i)
+            x_copy(i, "s")
+
+        blocks = [(h, c) for h in range(MH) for c in range(FC)]
+
+        def y_s(n, pieces):
+            for w in pieces:
+                y_group(*blocks[n], w * P, w * P + P, "s")
+
+        def stt(n, t):
+            s1_out(*blocks[n], t)
+
+        def p(n):
+            for t in range(4):
+                s1_mm(*blocks[n], t)
+
+        def ht(n, engines="ss"):
+            for half in range(2):
+                z_transpose(*blocks[n], half)
+                z_copy(*blocks[n], half, engines[half])
+
+        for i in range(4):
+            xpre(i)
+            e_s(0, 0, [i])
+        e_v(1, 0)
+        nc.scalar.activation(
+            out=amp_abs[:].rearrange("p (h e n) -> p h e n", h=MH, e=2),
+            in_=amp_sb[:].rearrange("p (h n e) -> p h e n", h=MH, e=2),
+            func=ACT.Abs,
+        )
+        e_quant(0, 0)
+        x_quant(0, 0)
+        x_quant(0, 1)
+        e_quant(1, 0)
+        e_v(1, 1)
+        p(0)
+        e_s(0, 1)
+        e_s(0, 2)
+        stt(0, 0)
+        stt(0, 1)
+        stt(0, 2)
+        stt(0, 3)
+        xpre(4)
+        relu(*blocks[0])
+        e_quant(0, 1)
+        e_quant(1, 1)
+        p(1)
+        y_s(0, [0, 1])
+        ht(0)
+        y_s(0, [2, 3])
+        xpre(5)
+        stt(1, 0)
+        stt(1, 1)
+        e_v(1, 2)
+        stt(1, 2)
+        z_quant(0, 0)
+        stt(1, 3)
+        y_quant(0, 0)
+        relu(*blocks[1])
+        e_quant(0, 2)
+        e_quant(1, 2)
+        p(2)
+        y_s(1, [0, 1])
+        ht(1)
+        y_s(1, [2, 3])
+        xpre(6)
+        stt(2, 0)
+        stt(2, 1)
+        xpre(7)
+        stt(2, 2)
+        z_quant(0, 1)
+        stt(2, 3)
+        y_quant(0, 1)
+        relu(*blocks[2])
+        x_quant(1, 0)
+        x_quant(1, 1)
+        nc.scalar.activation(out=sgn_z[:], in_=amp_zs[:], func=ACT.Sign)
+        sp = psum.tile([P, M // P, P], BF16, name="tp", bufs=2)
+        for i in range(M // P):
+            nc.tensor.transpose(sp[:, i, :], amp_sb[:, KP * (i // 4) + 2 * P * (i % 2) + (i % 4) // 2 : KP * (i // 4) + 2 * P * (i % 2) + 2 * P : 2], ident_bf[:])
+        nc.scalar.activation(out=sgn_y[:], in_=sp[:, :, 0:1].rearrange("p i o -> p (i o)"), func=ACT.Sign)
+        p(3)
+        y_s(2, [0, 1])
+        ht(2)
+        y_s(2, [2, 3])
+        a_sign(0)
+        stt(3, 0)
+        stt(3, 1)
+        a_sign(1)
+        stt(3, 2)
+        z_quant(0, 2)
+        stt(3, 3)
+        y_quant(0, 2)
+        relu(*blocks[3])
+        p(4)
+        y_s(3, [0, 1])
+        ht(3)
+        y_s(3, [2, 3])
+        for w in range(4):
+            a_group(0, w * P, w * P + P, "s")
+        for i in range(2):
+            for n in range(2):
+                y_mm(i, n, (0, 1, 2))
+                y_out(i, n, "s")
+        stt(4, 0)
+        stt(4, 1)
+        stt(4, 2)
+        z_quant(1, 0)
+        stt(4, 3)
+        y_quant(1, 0)
+        relu(*blocks[4])
+        a_quant(0)
+        for w in range(4):
+            a_group(1, w * P, w * P + P, "s")
+        p(5)
+        y_s(4, [0, 1])
+        ht(4)
+        y_s(4, [2, 3])
+        for i in range(2, 4):
+            for n in range(2):
+                y_mm(i, n, (0, 1, 2))
+                y_out(i, n, "s")
+        stt(5, 0)
+        a_quant(1)
+        stt(5, 1)
+        z_quant(1, 1)
+        stt(5, 2)
+        y_quant(1, 1)
+        stt(5, 3)
+        for t in range(4):
+            z_mm(0, t)
+            z_out(0, t, "sv"[t % 2])
+        relu(*blocks[5])
+        for i in range(4, 7):
+            for n in range(2):
+                y_mm(i, n, (0, 1))
+        ht(5, "sv")
+        y_group(1, 2, 0, 128, "s")
+        y_group(1, 2, 128, 512, "v")
+        y_quant(1, 2)
+        z_quant(1, 2)
+        for i in range(4, 7):
+            for n in range(2):
+                y_mm(i, n, (2,))
+                y_out(i, n, "sv"[n])
+        for c in (1, 2):
+            for t in range(4):
+                z_mm(c, t)
+                z_out(c, t, "sv"[t % 2])
+        for n in range(2):
+            y_mm(7, n, (0, 1, 2))
+            y_out(7, n, "sv"[n])

@@ -3,13 +3,13 @@ from contextlib import ExitStack
 import concourse.mybir as mybir
 from concourse.masks import make_identity
 
-M, K, F, C, R = 1024, 1024, 1536, 1024, 512
-FLOPS = 2 * M * K * F + 2 * M * F * C + 2 * F * M * R
+SAMPLES, CHANNELS, ATOMS, READOUTS, ATTRIBUTES = 1024, 1024, 1536, 1024, 512
+FLOPS = 2 * SAMPLES * CHANNELS * ATOMS + 2 * SAMPLES * ATOMS * READOUTS + 2 * ATOMS * SAMPLES * ATTRIBUTES
 
 F32 = mybir.dt.float32
 BF16 = mybir.dt.bfloat16
-U32 = mybir.dt.uint32
 I32 = mybir.dt.int32
+U32 = mybir.dt.uint32
 U8 = mybir.dt.uint8
 FP8 = mybir.dt.float8_e4m3fn
 FP8X4 = mybir.dt.float8_e4m3fn_x4
@@ -18,91 +18,64 @@ ALU = mybir.AluOpType
 ACT = mybir.ActivationFunctionType
 
 P = 128
-KP = 512
-XP = K // KP
-FC = F // KP
-MH = M // KP
+SLOTS = 4
+PASS = P * SLOTS
+DEPTHS = CHANNELS // PASS
+CHUNKS = ATOMS // PASS
+HALVES = SAMPLES // PASS
+TILES = PASS // P
+SPREAD = 8
 
 
-def tile_relu_dictionary_readout_s8_kernel(tc, x_bytes, x_scale, enc, bias, amp, d_words, d_scales, attr, out_0, out_1):
+def tile_relu_dictionary_readout_s8_kernel(
+    tc, x_bytes, x_scale, enc, bias, amp, d_words, d_scales, attr, out_0, out_1
+):
     nc = tc.nc
     with ExitStack() as ctx:
         keep = ctx.enter_context(tc.tile_pool(name="keep", bufs=1))
         work = ctx.enter_context(tc.tile_pool(name="work", bufs=2))
         psum = ctx.enter_context(tc.psum_pool(name="psum", bufs=1))
+        ctx.enter_context(tc.manual_schedule())
 
         def kept(shape, dtype, name):
             return keep.tile(shape, dtype, name=name, align_bytes=64)
 
-        def cols(count, name):
-            return kept([P, count], U32, "%s_codes" % name), kept([P, count], U8, "%s_scales" % name)
+        def staged(shape, dtype, name, bufs):
+            return work.tile(shape, dtype, name=name, align_bytes=64, bufs=bufs)
 
-        scale_sb = kept([P, K], F32, "scale_sb")
-        x_sb = [kept([P, 4, K], U8, "x_sb%d" % h) for h in range(MH)]
-        enc_sb = [[kept([P, 4, KP], BF16, "enc_sb%d%d" % (g, c)) for c in range(FC)] for g in range(XP)]
-        bias_sb = kept([P, FC, 4], BF16, "bias_sb")
-        amp_zs = kept([P, MH, 4], BF16, "amp_zs")
-        amp_sb = kept([P, M], BF16, "amp_sb")
-        d_sb = kept([P, FC, 2 * C], U8, "d_sb")
-        ds_sb = kept([P, FC, C], U8, "ds_sb")
-        attr_sb = [kept([P, 4, R], BF16, "attr_sb%d" % h) for h in range(MH)]
+        def product_bank(shape=(P, PASS)):
+            return psum.tile(list(shape), F32, name="product", bufs=6)
 
-        xv = x_bytes.rearrange("(h s p e) k -> h e p s k", h=MH, s=2, e=2)
-        ev = enc.rearrange("(g p j) f -> g p j f", p=P, j=4)
-        av = attr.rearrange("(h p u) r -> h p u r", p=P, u=4)
+        def transpose_bank(shape, dtype=F32):
+            return psum.tile(shape, dtype, name="transposed", bufs=2)
 
-        def load_enc(g, c):
-            nc.sync.dma_start(out=enc_sb[g][c][:], in_=ev[g][:, :, c * KP : (c + 1) * KP])
+        def mx_operand(name):
+            return kept([P, PASS], U32, name + "_codes"), kept([P, PASS], U8, name + "_scales")
 
-        nc.gpsimd.memset(ds_sb[:].rearrange("p g n -> p (g n)").bitcast(I32), 0)
-        nc.sync.dma_start(out=scale_sb[:], in_=x_scale.rearrange("o k -> (o k)").partition_broadcast(P))
-        nc.sync.dma_start(out=x_sb[0][:, 0:2, :], in_=xv[0][0])
-        load_enc(0, 0)
-        nc.sync.dma_start(out=x_sb[0][:, 2:4, :], in_=xv[0][1])
-        load_enc(1, 0)
-        nc.sync.dma_start(out=amp_sb[:], in_=amp.partition_broadcast(P))
-        nc.sync.dma_start(out=bias_sb[:], in_=bias.rearrange("(c p t) -> p c t", p=P, t=4))
-        load_enc(0, 1)
-        load_enc(1, 1)
-        for e in range(2):
-            nc.sync.dma_start(out=x_sb[1][:, 2 * e : 2 * e + 2, :], in_=xv[1][e])
-        load_enc(0, 2)
-        load_enc(1, 2)
-        nc.sync.dma_start(out=amp_zs[:], in_=amp.rearrange("(h p u) -> p h u", p=P, u=4))
-        nc.sync.dma_start(out=d_sb[:], in_=d_words.rearrange("g p n -> p g n"))
-        for q in range(4):
-            nc.sync.dma_start(
-                out=ds_sb[32 * q : 32 * q + 4, :, :].bitcast(I32),
-                in_=d_scales[:, 4 * q : 4 * q + 4, :].rearrange("g q n -> q g n").bitcast(I32),
+        def quantize(operand, grouped):
+            codes, scales = operand
+            nc.vector.quantize_mx(
+                out=codes[:].bitcast(FP8X4), scales=scales[:], in_=grouped[:].rearrange("p n j -> p (n j)")
             )
-        for h in range(MH):
-            nc.sync.dma_start(out=attr_sb[h][:], in_=av[h])
 
-        ident = kept([P, P], F32, "ident")
-        make_identity(nc, ident[:])
-        ident_bf = kept([P, P], BF16, "ident_bf")
-        nc.gpsimd.tensor_copy(out=ident_bf[:], in_=ident[:])
+        def multiply(out, stationary, columns, moving, start, stop):
+            codes, scales = stationary
+            nc.tensor.matmul_mx(
+                out=out,
+                lhsT=codes[:, columns].bitcast(FP8X4),
+                lhsT_scale=scales[:, columns],
+                rhs=moving[0],
+                rhs_scale=moving[1],
+                start=start,
+                stop=stop,
+            )
 
-        x_q = [[cols(KP, "x%d%d" % (h, g)) for g in range(XP)] for h in range(MH)]
-        e_q = [[cols(KP, "e%d%d" % (g, c)) for c in range(FC)] for g in range(XP)]
-        a_q = [cols(R, "a%d" % h) for h in range(MH)]
-        y_q = [[cols(KP, "y%d%d" % (h, c)) for c in range(FC)] for h in range(MH)]
-        z_q = [[cols(KP, "z%d%d" % (h, c)) for c in range(FC)] for h in range(MH)]
-        amp_abs = kept([P, M], BF16, "amp_abs")
-        sgn_z = kept([P, MH, 4], F32, "sgn_z")
-        sgn_y = kept([P, M // P], F32, "sgn_y")
+        def moved(operand):
+            codes, scales = operand
+            return codes[:].bitcast(FP8X4), scales[:]
 
-        x_grp = [None] * MH
-        e_grp = {}
-        a_sgn = {}
-        a_grp = {}
-        h_raw = {}
-        h_relu = {}
-        y_grp = {}
-        z_grp = {}
-
-        def quantize(pair, grouped):
-            nc.vector.quantize_mx(out=pair[0][:].bitcast(FP8X4), scales=pair[1][:], in_=grouped[:].rearrange("p w j -> p (w j)"))
+        def columns_of(t):
+            return slice(P * t, P * (t + 1))
 
         def copy(engine, out, in_):
             if engine == "s":
@@ -110,331 +83,473 @@ def tile_relu_dictionary_readout_s8_kernel(tc, x_bytes, x_scale, enc, bias, amp,
             else:
                 nc.vector.tensor_copy(out=out, in_=in_)
 
-        xbf = {}
+        identity = kept([P, P], F32, "identity")
+        make_identity(nc, identity[:])
+        identity_bf = kept([P, P], BF16, "identity_bf")
+        nc.gpsimd.tensor_copy(out=identity_bf[:], in_=identity[:])
+        d_scales_sb = kept([P, CHUNKS, READOUTS], U8, "d_scales_sb")
+        nc.gpsimd.memset(d_scales_sb[:].rearrange("p c n -> p (c n)").bitcast(I32), 0)
 
-        def x_product(i):
-            xbf[i] = work.tile([P, K], BF16, name="xbf", align_bytes=64, bufs=3)
-            nc.vector.tensor_tensor(out=xbf[i][:], in0=x_sb[i // 4][:, i % 4, :].bitcast(FP8), in1=scale_sb[:], op=ALU.mult)
+        scale_spread = kept([P, SPREAD], F32, "scale_spread")
+        amp_spread = kept([P, SPREAD], BF16, "amp_spread")
+        x_sb = [kept([P, 2, 2, CHANNELS], U8, "x_sb%d" % h) for h in range(HALVES)]
+        enc_sb = [[kept([P, SLOTS, PASS], BF16, "enc_sb%d%d" % (g, c)) for c in range(CHUNKS)] for g in range(DEPTHS)]
+        bias_sb = kept([P, CHUNKS, TILES], BF16, "bias_sb")
+        amp_y = kept([P, HALVES, 2, 2], BF16, "amp_y")
+        amp_attr = kept([P, HALVES, SLOTS], BF16, "amp_attr")
+        d_sb = kept([P, CHUNKS, 2 * READOUTS], U8, "d_sb")
+        attr_sb = [kept([P, SLOTS, ATTRIBUTES], BF16, "attr_sb%d" % h) for h in range(HALVES)]
 
-        xt = {}
+        x_rows = x_bytes.rearrange("(h s p e) k -> h p s (e k)", h=HALVES, s=2, e=2)
+        enc_rows = enc.rearrange("(g p j) f -> g p j f", p=P, j=SLOTS)
+        attr_rows = attr.rearrange("(h p v) r -> h p v r", p=P, v=SLOTS)
 
-        def x_transpose(i):
-            words = xbf[i][:].bitcast(F32)
-            xt[i] = psum.tile([P, XP, 2, P], F32, name="tp", bufs=2)
-            for g in range(XP):
-                for u in range(2):
-                    nc.tensor.transpose(xt[i][:, g, u, :], words[:, 256 * g + u : 256 * (g + 1) : 2], ident[:])
+        def load_enc(g, c):
+            nc.sync.dma_start(out=enc_sb[g][c][:], in_=enc_rows[g][:, :, c * PASS : (c + 1) * PASS])
 
-        def x_copy(i, engine):
-            h, r = divmod(i, 4)
-            if r == 0:
-                x_grp[h] = work.tile([P, XP, KP, 4], BF16, name="x_grp", align_bytes=64, bufs=1)
-            dst = x_grp[h][:].rearrange("p g r j -> p (g r j)").bitcast(F32).rearrange("p (g r u) -> p g r u", g=XP, u=2)
-            copy(engine, dst[:, :, P * r : P * (r + 1), :], xt[i][:].rearrange("p g u r -> p g r u"))
-
-        def x_quant(h, g):
-            quantize(x_q[h][g], x_grp[h][:, g, :, :])
-
-        def e_group(g, c, t0, t1, engine):
-            if t0 == 0:
-                e_grp[g, c] = work.tile([P, KP, 4], BF16, name="e_grp", align_bytes=64, bufs=3)
-            dst = e_grp[g, c][:].rearrange("p (t m) j -> p t m j", t=4)
-            src = enc_sb[g][c][:].rearrange("p j (m t) -> p t m j", t=4)
-            copy(engine, dst[:, t0:t1], src[:, t0:t1])
-
-        def e_quant(g, c):
-            quantize(e_q[g][c], e_grp[g, c])
-
-        def a_sign(h):
-            a_sgn[h] = work.tile([P, 4, R], BF16, name="a_sgn", align_bytes=64, bufs=2)
-            for u in range(4):
-                nc.vector.tensor_scalar_mul(a_sgn[h][:, u, :], attr_sb[h][:, u, :], sgn_z[:, h, u : u + 1])
-
-        def interleave(dst, src, w0, w1, engine):
-            copy(
-                engine,
-                dst[:, w0:w1, :].rearrange("p (c i) t -> p c t i", i=4),
-                src[:, :, w0:w1].rearrange("p t (c i) -> p c t i", i=4),
+        nc.sync.dma_start(out=scale_spread[:], in_=x_scale.rearrange("o (p c) -> p (o c)", c=SPREAD))
+        nc.sync.dma_start(out=amp_spread[:], in_=amp.rearrange("(p c) -> p c", c=SPREAD))
+        nc.sync.dma_start(out=x_sb[0][:, 0].rearrange("p e k -> p (e k)"), in_=x_rows[0][:, 0])
+        load_enc(0, 0)
+        nc.sync.dma_start(out=x_sb[0][:, 1].rearrange("p e k -> p (e k)"), in_=x_rows[0][:, 1])
+        load_enc(1, 0)
+        load_enc(0, 1)
+        load_enc(1, 1)
+        nc.sync.dma_start(out=x_sb[1][:].rearrange("p s e k -> p s (e k)"), in_=x_rows[1])
+        nc.sync.dma_start(out=bias_sb[:], in_=bias.rearrange("(c p t) -> p c t", p=P, t=TILES))
+        load_enc(0, 2)
+        load_enc(1, 2)
+        nc.sync.dma_start(out=amp_y[:], in_=amp.rearrange("(h s p e) -> p h s e", h=HALVES, s=2, e=2))
+        nc.sync.dma_start(out=amp_attr[:], in_=amp.rearrange("(h p v) -> p h v", p=P, v=SLOTS))
+        nc.sync.dma_start(out=d_sb[:], in_=d_words.rearrange("c p n -> p c n"))
+        for quadrant in range(4):
+            nc.sync.dma_start(
+                out=d_scales_sb[32 * quadrant : 32 * quadrant + 4, :, :].bitcast(I32),
+                in_=d_scales[:, 4 * quadrant : 4 * quadrant + 4, :].rearrange("c q n -> q c n").bitcast(I32),
             )
+        for h in range(HALVES):
+            nc.sync.dma_start(out=attr_sb[h][:], in_=attr_rows[h])
 
-        def a_group(h, w0, w1, engine):
-            if w0 == 0:
-                a_grp[h] = work.tile([P, R, 4], BF16, name="a_grp", align_bytes=64, bufs=1)
-            copy(
-                engine,
-                a_grp[h][:, w0:w1, :].rearrange("p r (u e) -> p r u e", u=2),
-                a_sgn[h][:, :, w0:w1].rearrange("p (e u) r -> p r u e", e=2),
-            )
+        x_mx = [[mx_operand("x%d%d" % (h, g)) for g in range(DEPTHS)] for h in range(HALVES)]
+        enc_mx = [[mx_operand("enc%d%d" % (g, c)) for c in range(CHUNKS)] for g in range(DEPTHS)]
+        attr_mx = [mx_operand("attr%d" % h) for h in range(HALVES)]
+        hy_mx = [[mx_operand("hy%d%d" % (h, c)) for c in range(CHUNKS)] for h in range(HALVES)]
+        hz_mx = [[mx_operand("hz%d%d" % (h, c)) for c in range(CHUNKS)] for h in range(HALVES)]
+        scale_sb = kept([P, CHANNELS], F32, "scale_sb")
+        amp_abs = kept([P, SAMPLES], BF16, "amp_abs")
+        sign_y = kept([P, HALVES * TILES], F32, "sign_y")
+        sign_attr = kept([P, HALVES, SLOTS], F32, "sign_attr")
 
-        def a_quant(h):
-            quantize(a_q[h], a_grp[h])
+        widened, x_turned, x_grouped, enc_grouped = {}, {}, {}, {}
+        attr_signed, attr_grouped = {}, {}
+        pre, h_signed, h_sb, hy_grouped, hz_turned, hz_grouped = {}, {}, {}, {}, {}, {}
+        y_sums, z_sums = {}, {}
 
-        pre = {}
+        def made(table, key, shape, name, bufs):
+            if key not in table:
+                table[key] = staged(shape, BF16, name, bufs)
+            return table[key]
 
-        def s1_mm(h, c, t):
-            pre[h, c, t] = psum.tile([P, KP], F32, name="mm", bufs=6)
-            for g in range(XP):
-                nc.tensor.matmul_mx(
-                    out=pre[h, c, t][:],
-                    lhsT=e_q[g][c][0][:, P * t : P * (t + 1)].bitcast(FP8X4),
-                    lhsT_scale=e_q[g][c][1][:, P * t : P * (t + 1)],
-                    rhs=x_q[h][g][0][:].bitcast(FP8X4),
-                    rhs_scale=x_q[h][g][1][:],
-                    start=(g == 0),
-                    stop=(g == XP - 1),
+        zeros = kept([P, PASS], BF16, "zeros")
+        nc.vector.memset(zeros[:], 0.0)
+        unread = product_bank()
+
+        def keep_awake(*moving):
+            for rhs in moving:
+                nc.tensor.matmul(unread[:], lhsT=identity_bf[:], rhs=rhs, start=True, stop=True)
+
+        def first_columns(g, c):
+            return enc_grouped[g, c][:, :P, :].rearrange("p n j -> p (n j)")
+
+        def spread_scale():
+            for bank, engine in enumerate("sv"):
+                rows = transpose_bank([P, 4, P])
+                for c in range(4):
+                    column = scale_spread[:, 4 * bank + c : 4 * bank + c + 1]
+                    nc.tensor.transpose(rows[:, c, :], column.to_broadcast([P, P]), identity[:])
+                by_c = scale_sb[:].rearrange("p (i c) -> p i c", c=SPREAD)
+                copy(engine, by_c[:, :, 4 * bank : 4 * bank + 4], rows[:].rearrange("p c i -> p i c"))
+
+        def spread_amp():
+            rows = transpose_bank([P, SPREAD, P], BF16)
+            for c in range(SPREAD):
+                nc.tensor.transpose(rows[:, c, :], amp_spread[:, c : c + 1].to_broadcast([P, P]), identity_bf[:])
+            for h in range(HALVES):
+                nc.scalar.activation(
+                    out=amp_abs[:, PASS * h : PASS * (h + 1)].rearrange("p (e i m) -> p e i m", e=2, m=4),
+                    in_=rows[:, :, 64 * h : 64 * (h + 1)].rearrange("p (m e) i -> p e i m", e=2),
+                    func=ACT.Abs,
                 )
 
-        def s1_out(h, c, t):
-            if t == 0:
-                h_raw[h, c] = work.tile([P, 4, KP], BF16, name="h_raw", align_bytes=64, bufs=3)
-            nc.vector.scalar_tensor_tensor(
-                out=h_raw[h, c][:, t, :],
-                in0=pre[h, c, t][:],
-                scalar=bias_sb[:, c, t : t + 1],
-                in1=amp_abs[:, KP * h : KP * (h + 1)],
-                op0=ALU.add,
-                op1=ALU.mult,
+        def take_signs():
+            nc.scalar.activation(out=sign_attr[:], in_=amp_attr[:], func=ACT.Sign)
+            nc.scalar.activation(
+                out=sign_y[:].rearrange("p (h e s) -> p h e s", h=HALVES, e=2),
+                in_=amp_y[:].rearrange("p h s e -> p h e s"),
+                func=ACT.Sign,
             )
+
+        def widen_x(*tiles):
+            for i in tiles:
+                h, e, s = i // 4, i % 4 // 2, i % 2
+                widened[i] = staged([P, CHANNELS], BF16, "widened", 3)
+                nc.vector.tensor_tensor(
+                    out=widened[i][:], in0=x_sb[h][:, s, e, :].bitcast(FP8), in1=scale_sb[:], op=ALU.mult
+                )
+
+        def turn_x(i):
+            words = widened[i][:].bitcast(F32)
+            x_turned[i] = transpose_bank([P, DEPTHS, 2, P])
+            for g in range(DEPTHS):
+                for u in range(2):
+                    nc.tensor.transpose(
+                        x_turned[i][:, g, u, :], words[:, 256 * g + u : 256 * (g + 1) : 2], identity[:]
+                    )
+
+        def empty_x(i, engine):
+            h, tile = i // 4, i % 4
+            grouped = made(x_grouped, h, [P, DEPTHS, PASS, SLOTS], "x_grouped", 1)
+            words = grouped[:].rearrange("p g n j -> p (g n j)").bitcast(F32)
+            words = words.rearrange("p (g n u) -> p g n u", g=DEPTHS, u=2)
+            copy(engine, words[:, :, columns_of(tile), :], x_turned[i][:].rearrange("p g u n -> p g n u"))
+
+        def quantize_x(h, *depths):
+            for g in depths:
+                quantize(x_mx[h][g], x_grouped[h][:, g, :, :])
+
+        def group_enc(g, c, engine, *pieces):
+            grouped = made(enc_grouped, (g, c), [P, PASS, SLOTS], "enc_grouped", 4)
+            dst = grouped[:].rearrange("p (t a b) j -> p a j b t", t=TILES, b=2)
+            src = enc_sb[g][c][:].rearrange("p j (a b t) -> p a j b t", b=2, t=TILES)
+            for piece in pieces:
+                a = slice(16 * piece, 16 * (piece + 1))
+                copy(engine, dst[:, a], src[:, a])
+
+        def quantize_enc(g, c):
+            quantize(enc_mx[g][c], enc_grouped[g, c])
+
+        def sign_rows(h, *rows):
+            signed = made(attr_signed, h, [P, SLOTS, ATTRIBUTES], "attr_signed", 2)
+            for v in rows:
+                nc.vector.tensor_scalar_mul(signed[:, v, :], attr_sb[h][:, v, :], sign_attr[:, h, v : v + 1])
+
+        def group_attr(h, engine, *pieces):
+            grouped = made(attr_grouped, h, [P, ATTRIBUTES, SLOTS], "attr_grouped", 1)
+            for piece in pieces:
+                n = columns_of(piece)
+                copy(
+                    engine,
+                    grouped[:, n, :].rearrange("p (c i) (u e) -> p c e u i", i=4, u=2),
+                    attr_signed[h][:, :, n].rearrange("p (e u) (c i) -> p c e u i", i=4, e=2),
+                )
+
+        def quantize_attr(h):
+            quantize(attr_mx[h], attr_grouped[h])
+
+        def encode(h, c, *tiles):
+            for t in tiles:
+                pre[h, c, t] = product_bank()
+                for g in range(DEPTHS):
+                    multiply(
+                        pre[h, c, t][:], enc_mx[g][c], columns_of(t), moved(x_mx[h][g]), g == 0, g == DEPTHS - 1
+                    )
+
+        def scale_h(h, c, *tiles):
+            signed = made(h_signed, (h, c), [P, TILES, PASS], "h_signed", 3)
+            for t in tiles:
+                nc.vector.scalar_tensor_tensor(
+                    out=signed[:, t, :],
+                    in0=pre[h, c, t][:],
+                    scalar=bias_sb[:, c, t : t + 1],
+                    in1=amp_abs[:, PASS * h : PASS * (h + 1)],
+                    op0=ALU.add,
+                    op1=ALU.mult,
+                )
 
         def relu(h, c):
-            h_relu[h, c] = work.tile([P, 4, KP], BF16, name="h_relu", align_bytes=64, bufs=3)
-            nc.vector.tensor_scalar_max(h_relu[h, c][:], h_raw[h, c][:], 0.0)
+            rectified = made(h_sb, (h, c), [P, TILES, PASS], "h_sb", 3)
+            nc.vector.tensor_scalar_max(rectified[:], h_signed[h, c][:], 0.0)
 
-        def y_group(h, c, w0, w1, engine):
-            if w0 == 0:
-                y_grp[h, c] = work.tile([P, KP, 4], BF16, name="y_grp", align_bytes=64, bufs=3)
-            interleave(y_grp[h, c], h_relu[h, c], w0, w1, engine)
-
-        def y_quant(h, c):
-            quantize(y_q[h][c], y_grp[h, c])
-
-        zt = {}
-
-        def z_transpose(h, c, half):
-            zt[h, c, half] = psum.tile([P, 2, 2, P], F32, name="tp", bufs=2)
-            for tt in range(2):
-                words = h_relu[h, c][:, 2 * half + tt, :].bitcast(F32)
-                for u in range(2):
-                    nc.tensor.transpose(zt[h, c, half][:, tt, u, :], words[:, P * u : P * (u + 1)], ident[:])
-
-        def z_copy(h, c, half, engine):
-            if half == 0:
-                z_grp[h, c] = work.tile([P, KP, 4], BF16, name="z_grp", align_bytes=64, bufs=3)
-            dst = z_grp[h, c][:].rearrange("p n j -> p (n j)").bitcast(F32).rearrange("p (t n u) -> p t n u", t=4, u=2)
-            copy(engine, dst[:, 2 * half : 2 * half + 2], zt[h, c, half][:].rearrange("p t u n -> p t n u"))
-
-        def z_quant(h, c):
-            quantize(z_q[h][c], z_grp[h, c])
-
-        y_acc = {}
-        y_sb = {}
-
-        def y_mm(i, n, passes):
-            h, r = divmod(i, 4)
-            if passes[0] == 0:
-                y_acc[i, n] = psum.tile([P, KP], F32, name="mm", bufs=6)
-            for c in passes:
-                nc.tensor.matmul_mx(
-                    out=y_acc[i, n][:],
-                    lhsT=y_q[h][c][0][:, P * r : P * (r + 1)].bitcast(FP8X4),
-                    lhsT_scale=y_q[h][c][1][:, P * r : P * (r + 1)],
-                    rhs=d_sb[:, c, 2 * KP * n : 2 * KP * (n + 1)].bitcast(FP4X4),
-                    rhs_scale=ds_sb[:, c, KP * n : KP * (n + 1)],
-                    start=(c == 0),
-                    stop=(c == FC - 1),
+        def group_hy(h, c, engine, *pieces):
+            grouped = made(hy_grouped, (h, c), [P, PASS, SLOTS], "hy_grouped", 3)
+            for piece in pieces:
+                n = columns_of(piece)
+                copy(
+                    engine,
+                    grouped[:, n, :].rearrange("p (c i) t -> p c t i", i=4),
+                    h_sb[h, c][:, :, n].rearrange("p t (c i) -> p c t i", i=4),
                 )
 
-        yv = out_0.rearrange("(h s p e) c -> h e s p c", h=MH, s=2, e=2)
+        def quantize_hy(h, c):
+            quantize(hy_mx[h][c], hy_grouped[h, c])
 
-        def y_out(i, n, engine):
-            h, r = divmod(i, 4)
-            sb = work.tile([P, KP], F32, name="y_sb", bufs=6)
+        def turn_hz(h, c, *pairs):
+            for pair in pairs:
+                hz_turned[h, c, pair] = transpose_bank([P, 2, 2, P])
+                for k in range(2):
+                    words = h_sb[h, c][:, 2 * pair + k, :].bitcast(F32)
+                    for u in range(2):
+                        nc.tensor.transpose(
+                            hz_turned[h, c, pair][:, k, u, :], words[:, columns_of(u)], identity[:]
+                        )
+
+        def empty_hz(h, c, pair, engine):
+            grouped = made(hz_grouped, (h, c), [P, PASS, SLOTS], "hz_grouped", 3)
+            words = grouped[:].rearrange("p n j -> p (n j)").bitcast(F32)
+            words = words.rearrange("p (t n u) -> p t n u", t=TILES, u=2)
+            copy(
+                engine,
+                words[:, 2 * pair : 2 * pair + 2],
+                hz_turned[h, c, pair][:].rearrange("p t u n -> p t n u"),
+            )
+
+        def quantize_hz(h, c):
+            quantize(hz_mx[h][c], hz_grouped[h, c])
+
+        y_rows = out_0.rearrange("(h s p e) c -> h e s p c", h=HALVES, s=2, e=2)
+
+        def read_out(i, n, *chunks):
+            if chunks[0] == 0:
+                y_sums[i, n] = product_bank()
+            for c in chunks:
+                d = (
+                    d_sb[:, c, 2 * PASS * n : 2 * PASS * (n + 1)].bitcast(FP4X4),
+                    d_scales_sb[:, c, PASS * n : PASS * (n + 1)],
+                )
+                multiply(y_sums[i, n][:], hy_mx[i // 4][c], columns_of(i % 4), d, c == 0, c == CHUNKS - 1)
+
+        def store_y(i, n, engine):
+            result = work.tile([P, PASS], F32, name="y_result", bufs=8)
+            sign = sign_y[:, i : i + 1]
             if engine == "s":
-                nc.scalar.activation(out=sb[:], in_=y_acc[i, n][:], func=ACT.Copy, scale=sgn_y[:, i : i + 1])
+                nc.scalar.activation(out=result[:], in_=y_sums[i, n][:], func=ACT.Copy, scale=sign)
             else:
-                nc.vector.tensor_scalar_mul(sb[:], y_acc[i, n][:], sgn_y[:, i : i + 1])
-            nc.sync.dma_start(out=yv[h][r // 2][r % 2][:, KP * n : KP * (n + 1)], in_=sb[:])
+                nc.vector.tensor_scalar_mul(result[:], y_sums[i, n][:], sign)
+            rows = y_rows[i // 4][i % 4 // 2][i % 2]
+            nc.sync.dma_start(out=rows[:, PASS * n : PASS * (n + 1)], in_=result[:])
 
-        zv = out_1.rearrange("(c p t) r -> c t p r", p=P, t=4)
-        z_acc = {}
+        z_rows = out_1.rearrange("(c p t) r -> c t p r", p=P, t=TILES)
 
-        def z_mm(c, t):
-            z_acc[c, t] = psum.tile([P, R], F32, name="mm", bufs=6)
-            for h in range(MH):
-                nc.tensor.matmul_mx(
-                    out=z_acc[c, t][:],
-                    lhsT=z_q[h][c][0][:, P * t : P * (t + 1)].bitcast(FP8X4),
-                    lhsT_scale=z_q[h][c][1][:, P * t : P * (t + 1)],
-                    rhs=a_q[h][0][:].bitcast(FP8X4),
-                    rhs_scale=a_q[h][1][:],
-                    start=(h == 0),
-                    stop=(h == MH - 1),
-                )
+        def associate(c, *tiles):
+            for t in tiles:
+                z_sums[c, t] = product_bank()
+                for h in range(HALVES):
+                    multiply(
+                        z_sums[c, t][:], hz_mx[h][c], columns_of(t), moved(attr_mx[h]), h == 0, h == HALVES - 1
+                    )
 
-        def z_out(c, t, engine):
-            sb = work.tile([P, R], F32, name="z_sb", bufs=6)
-            copy(engine, sb[:], z_acc[c, t][:])
-            nc.sync.dma_start(out=zv[c][t], in_=sb[:])
+        def store_z(c, t, engine):
+            result = work.tile([P, ATTRIBUTES], F32, name="z_result", bufs=4)
+            copy(engine, result[:], z_sums[c, t][:])
+            nc.sync.dma_start(out=z_rows[c][t], in_=result[:])
 
-        def e_s(g, c, ts=range(4)):
-            for t in ts:
-                e_group(g, c, t, t + 1, "s")
+        spread_scale()
+        spread_amp()
+        keep_awake(zeros[:], zeros[:], zeros[:])
+        widen_x(0)
+        group_enc(0, 0, "s", 0, 2, 3)
+        group_enc(0, 0, "v", 1)
+        group_enc(1, 0, "s", 0)
+        widen_x(2, 1)
+        turn_x(0)
+        keep_awake(widened[0][:, :PASS])
+        turn_x(2)
+        keep_awake(widened[2][:, :PASS])
+        widen_x(3)
+        empty_x(2, "s")
+        group_enc(0, 1, "s", 0)
+        quantize_enc(0, 0)
+        empty_x(0, "s")
+        turn_x(3)
+        keep_awake(widened[3][:, :PASS])
+        group_enc(1, 0, "v", 1, 2, 3)
+        group_enc(1, 1, "s", 0)
+        group_enc(1, 1, "v", 1)
+        turn_x(1)
+        keep_awake(widened[1][:, :PASS], first_columns(0, 0), first_columns(1, 0))
+        empty_x(3, "s")
+        empty_x(1, "s")
+        quantize_enc(1, 0)
+        widen_x(4)
 
-        def e_v(g, c):
-            e_group(g, c, 0, 2, "v")
-            e_group(g, c, 2, 4, "v")
+        group_enc(1, 1, "s", 2)
+        group_enc(0, 1, "s", 1)
+        group_enc(1, 1, "s", 3)
+        group_enc(0, 1, "s", 3)
+        group_enc(0, 2, "s", 0)
+        quantize_x(0, 0, 1)
+        group_enc(0, 1, "v", 2)
+        group_enc(1, 2, "s", 0)
+        group_enc(0, 2, "s", 1, 2, 3)
+        encode(0, 0, 0, 1, 2, 3)
+        widen_x(5)
+        quantize_enc(1, 1)
+        quantize_enc(0, 1)
+        scale_h(0, 0, 0, 3, 1, 2)
+        encode(0, 1, 0, 1, 2, 3)
+        group_enc(1, 2, "s", 1, 2, 3)
+        quantize_enc(0, 2)
+        relu(0, 0)
+        scale_h(0, 1, 1)
+        group_hy(0, 0, "s", 0, 1)
+        turn_hz(0, 0, 0, 1)
+        quantize_enc(1, 2)
+        scale_h(0, 1, 3, 0, 2)
+        encode(0, 2, 0)
+        empty_hz(0, 0, 0, "s")
+        empty_hz(0, 0, 1, "s")
+        widen_x(6)
+        take_signs()
+        group_hy(0, 0, "s", 2, 3)
+        turn_x(4)
+        encode(0, 2, 1, 2, 3)
+        relu(0, 1)
+        empty_x(4, "s")
+        scale_h(0, 2, 0, 2, 3)
+        group_hy(0, 1, "s", 0, 1)
+        group_hy(0, 1, "v", 2)
+        turn_x(6)
+        turn_x(5)
+        empty_x(6, "s")
+        quantize_hy(0, 0)
+        group_hy(0, 1, "s", 3)
+        scale_h(0, 2, 1)
+        turn_hz(0, 1, 0)
+        empty_hz(0, 1, 0, "s")
+        quantize_hy(0, 1)
+        empty_x(5, "s")
+        relu(0, 2)
 
-        def xpre(i):
-            x_product(i)
-            x_transpose(i)
-            x_copy(i, "s")
+        read_out(0, 0, 0, 1)
+        read_out(0, 1, 0, 1)
+        read_out(1, 0, 0, 1)
+        read_out(1, 1, 0, 1)
+        sign_rows(0, 0, 1)
+        group_hy(0, 2, "s", 0, 1, 2)
+        widen_x(7)
+        sign_rows(0, 2)
+        group_hy(0, 2, "v", 3)
+        turn_hz(0, 2, 0)
+        sign_rows(0, 3)
+        quantize_hz(0, 0)
+        group_attr(0, "s", 0)
+        turn_x(7)
+        quantize_hy(0, 2)
+        read_out(2, 0, 0, 1)
+        read_out(2, 1, 0, 1)
+        read_out(2, 1, 2)
+        read_out(1, 1, 2)
+        read_out(0, 0, 2)
+        read_out(0, 1, 2)
+        read_out(1, 0, 2)
+        read_out(2, 0, 2)
+        empty_x(7, "s")
+        group_attr(0, "v", 1, 2)
+        sign_rows(1, 0)
+        store_y(2, 1, "s")
+        store_y(1, 1, "s")
+        store_y(1, 0, "s")
+        store_y(0, 0, "s")
+        quantize_x(1, 0, 1)
+        sign_rows(1, 1, 2)
 
-        blocks = [(h, c) for h in range(MH) for c in range(FC)]
+        encode(1, 0, 0, 1)
+        group_attr(0, "v", 3)
+        sign_rows(1, 3)
+        scale_h(1, 0, 0, 1)
+        turn_hz(0, 1, 1)
+        empty_hz(0, 1, 1, "s")
+        quantize_attr(0)
+        encode(1, 0, 2, 3)
+        encode(1, 1, 0, 1)
+        store_y(0, 1, "s")
+        scale_h(1, 0, 2, 3)
+        scale_h(1, 1, 0)
+        group_attr(1, "s", 0)
+        store_y(2, 0, "s")
+        empty_hz(0, 2, 0, "s")
+        relu(1, 0)
+        encode(1, 2, 0)
+        group_attr(1, "s", 1)
+        group_attr(1, "v", 2)
+        turn_hz(0, 2, 1)
+        group_hy(1, 0, "v", 0)
+        empty_hz(0, 2, 1, "s")
+        encode(1, 1, 2)
+        scale_h(1, 1, 1, 2)
+        group_attr(1, "s", 3)
+        turn_hz(1, 0, 0, 1)
+        group_hy(1, 0, "s", 1, 2)
+        quantize_hz(0, 1)
+        encode(1, 1, 3)
+        scale_h(1, 1, 3)
+        read_out(3, 0, 0, 1, 2)
+        read_out(3, 1, 0, 1, 2)
+        quantize_attr(1)
+        empty_hz(1, 0, 0, "s")
+        empty_hz(1, 0, 1, "s")
+        relu(1, 1)
+        quantize_hz(0, 2)
+        group_hy(1, 0, "s", 3)
+        encode(1, 2, 1, 2)
+        scale_h(1, 2, 0, 1)
+        store_y(3, 1, "s")
+        store_y(3, 0, "s")
+        turn_hz(1, 1, 0, 1)
+        quantize_hz(1, 0)
+        empty_hz(1, 1, 1, "s")
+        empty_hz(1, 1, 0, "s")
+        encode(1, 2, 3)
+        scale_h(1, 2, 2, 3)
 
-        def y_s(n, pieces):
-            for w in pieces:
-                y_group(*blocks[n], w * P, w * P + P, "s")
+        associate(0, 0, 1, 2)
+        group_hy(1, 1, "s", 0)
+        quantize_hz(1, 1)
+        store_z(0, 0, "s")
+        store_z(0, 1, "s")
+        store_z(0, 2, "s")
+        relu(1, 2)
+        associate(1, 0)
+        associate(0, 3)
+        associate(1, 1)
+        group_hy(1, 1, "v", 1)
+        group_hy(1, 2, "v", 0)
+        group_hy(1, 1, "v", 2)
+        group_hy(1, 1, "s", 3)
+        group_hy(1, 2, "v", 1)
+        group_hy(1, 2, "s", 2, 3)
+        quantize_hy(1, 0)
+        turn_hz(1, 2, 0, 1)
+        store_z(0, 3, "v")
+        store_z(1, 0, "s")
+        associate(1, 2, 3)
+        quantize_hy(1, 1)
+        quantize_hy(1, 2)
+        store_z(1, 3, "s")
+        empty_hz(1, 2, 0, "v")
 
-        def stt(n, t):
-            s1_out(*blocks[n], t)
-
-        def p(n):
-            for t in range(4):
-                s1_mm(*blocks[n], t)
-
-        def ht(n, engines="ss"):
-            for half in range(2):
-                z_transpose(*blocks[n], half)
-                z_copy(*blocks[n], half, engines[half])
-
-        for i in range(4):
-            xpre(i)
-            e_s(0, 0, [i])
-        e_v(1, 0)
-        nc.scalar.activation(
-            out=amp_abs[:].rearrange("p (h e n) -> p h e n", h=MH, e=2),
-            in_=amp_sb[:].rearrange("p (h n e) -> p h e n", h=MH, e=2),
-            func=ACT.Abs,
-        )
-        e_quant(0, 0)
-        x_quant(0, 0)
-        x_quant(0, 1)
-        e_quant(1, 0)
-        e_v(1, 1)
-        p(0)
-        e_s(0, 1)
-        e_s(0, 2)
-        stt(0, 0)
-        stt(0, 1)
-        stt(0, 2)
-        stt(0, 3)
-        xpre(4)
-        relu(*blocks[0])
-        e_quant(0, 1)
-        e_quant(1, 1)
-        p(1)
-        y_s(0, [0, 1])
-        ht(0)
-        y_s(0, [2, 3])
-        xpre(5)
-        stt(1, 0)
-        stt(1, 1)
-        e_v(1, 2)
-        stt(1, 2)
-        z_quant(0, 0)
-        stt(1, 3)
-        y_quant(0, 0)
-        relu(*blocks[1])
-        e_quant(0, 2)
-        e_quant(1, 2)
-        p(2)
-        y_s(1, [0, 1])
-        ht(1)
-        y_s(1, [2, 3])
-        xpre(6)
-        stt(2, 0)
-        stt(2, 1)
-        xpre(7)
-        stt(2, 2)
-        z_quant(0, 1)
-        stt(2, 3)
-        y_quant(0, 1)
-        relu(*blocks[2])
-        x_quant(1, 0)
-        x_quant(1, 1)
-        nc.scalar.activation(out=sgn_z[:], in_=amp_zs[:], func=ACT.Sign)
-        sp = psum.tile([P, M // P, P], BF16, name="tp", bufs=2)
-        for i in range(M // P):
-            nc.tensor.transpose(sp[:, i, :], amp_sb[:, KP * (i // 4) + 2 * P * (i % 2) + (i % 4) // 2 : KP * (i // 4) + 2 * P * (i % 2) + 2 * P : 2], ident_bf[:])
-        nc.scalar.activation(out=sgn_y[:], in_=sp[:, :, 0:1].rearrange("p i o -> p (i o)"), func=ACT.Sign)
-        p(3)
-        y_s(2, [0, 1])
-        ht(2)
-        y_s(2, [2, 3])
-        a_sign(0)
-        stt(3, 0)
-        stt(3, 1)
-        a_sign(1)
-        stt(3, 2)
-        z_quant(0, 2)
-        stt(3, 3)
-        y_quant(0, 2)
-        relu(*blocks[3])
-        p(4)
-        y_s(3, [0, 1])
-        ht(3)
-        y_s(3, [2, 3])
-        for w in range(4):
-            a_group(0, w * P, w * P + P, "s")
-        for i in range(2):
-            for n in range(2):
-                y_mm(i, n, (0, 1, 2))
-                y_out(i, n, "s")
-        stt(4, 0)
-        stt(4, 1)
-        stt(4, 2)
-        z_quant(1, 0)
-        stt(4, 3)
-        y_quant(1, 0)
-        relu(*blocks[4])
-        a_quant(0)
-        for w in range(4):
-            a_group(1, w * P, w * P + P, "s")
-        p(5)
-        y_s(4, [0, 1])
-        ht(4)
-        y_s(4, [2, 3])
-        for i in range(2, 4):
-            for n in range(2):
-                y_mm(i, n, (0, 1, 2))
-                y_out(i, n, "s")
-        stt(5, 0)
-        a_quant(1)
-        stt(5, 1)
-        z_quant(1, 1)
-        stt(5, 2)
-        y_quant(1, 1)
-        stt(5, 3)
-        for t in range(4):
-            z_mm(0, t)
-            z_out(0, t, "sv"[t % 2])
-        relu(*blocks[5])
-        for i in range(4, 7):
-            for n in range(2):
-                y_mm(i, n, (0, 1))
-        ht(5, "sv")
-        y_group(1, 2, 0, 128, "s")
-        y_group(1, 2, 128, 512, "v")
-        y_quant(1, 2)
-        z_quant(1, 2)
-        for i in range(4, 7):
-            for n in range(2):
-                y_mm(i, n, (2,))
-                y_out(i, n, "sv"[n])
-        for c in (1, 2):
-            for t in range(4):
-                z_mm(c, t)
-                z_out(c, t, "sv"[t % 2])
-        for n in range(2):
-            y_mm(7, n, (0, 1, 2))
-            y_out(7, n, "sv"[n])
+        read_out(4, 0, 0, 1, 2)
+        read_out(4, 1, 0, 1, 2)
+        read_out(5, 0, 0, 1, 2)
+        read_out(5, 1, 0, 1, 2)
+        store_z(1, 1, "v")
+        store_y(4, 0, "s")
+        empty_hz(1, 2, 1, "s")
+        store_z(1, 2, "v")
+        store_y(4, 1, "v")
+        store_y(5, 0, "v")
+        store_y(5, 1, "s")
+        read_out(6, 0, 0, 1, 2)
+        read_out(6, 1, 0, 1, 2)
+        read_out(7, 0, 0, 1, 2)
+        read_out(7, 1, 0, 1, 2)
+        store_y(6, 0, "v")
+        store_y(6, 1, "s")
+        store_y(7, 0, "s")
+        store_y(7, 1, "s")
+        quantize_hz(1, 2)
+        associate(2, 0, 1, 2, 3)
+        store_z(2, 0, "v")
+        store_z(2, 1, "v")
+        store_z(2, 2, "v")
+        store_z(2, 3, "s")

from contextlib import ExitStack

import concourse.mybir as mybir
from concourse.masks import make_identity

SAMPLES, CHANNELS, ATOMS, READOUTS, ATTRIBUTES = 1024, 1024, 1536, 1024, 512
FLOPS = 2 * SAMPLES * CHANNELS * ATOMS + 2 * SAMPLES * ATOMS * READOUTS + 2 * ATOMS * SAMPLES * ATTRIBUTES

F32 = mybir.dt.float32
BF16 = mybir.dt.bfloat16
I32 = mybir.dt.int32
U32 = mybir.dt.uint32
U8 = mybir.dt.uint8
FP8 = mybir.dt.float8_e4m3fn
FP8X4 = mybir.dt.float8_e4m3fn_x4
FP4X4 = mybir.dt.float4_e2m1fn_x4
ALU = mybir.AluOpType
ACT = mybir.ActivationFunctionType

P = 128
SLOTS = 4
PASS = P * SLOTS
DEPTHS = CHANNELS // PASS
CHUNKS = ATOMS // PASS
HALVES = SAMPLES // PASS
TILES = PASS // P
SPREAD = 8


def tile_relu_dictionary_readout_s8_kernel(
    tc, x_bytes, x_scale, enc, bias, amp, d_words, d_scales, attr, out_0, out_1
):
    nc = tc.nc
    with ExitStack() as ctx:
        keep = ctx.enter_context(tc.tile_pool(name="keep", bufs=1))
        work = ctx.enter_context(tc.tile_pool(name="work", bufs=2))
        psum = ctx.enter_context(tc.psum_pool(name="psum", bufs=1))
        ctx.enter_context(tc.manual_schedule())

        def kept(shape, dtype, name):
            return keep.tile(shape, dtype, name=name, align_bytes=64)

        def staged(shape, dtype, name, bufs):
            return work.tile(shape, dtype, name=name, align_bytes=64, bufs=bufs)

        def product_bank(shape=(P, PASS)):
            return psum.tile(list(shape), F32, name="product", bufs=6)

        def transpose_bank(shape, dtype=F32):
            return psum.tile(shape, dtype, name="transposed", bufs=2)

        def mx_operand(name):
            return kept([P, PASS], U32, name + "_codes"), kept([P, PASS], U8, name + "_scales")

        def quantize(operand, grouped):
            codes, scales = operand
            nc.vector.quantize_mx(
                out=codes[:].bitcast(FP8X4), scales=scales[:], in_=grouped[:].rearrange("p n j -> p (n j)")
            )

        def multiply(out, stationary, columns, moving, start, stop):
            codes, scales = stationary
            nc.tensor.matmul_mx(
                out=out,
                lhsT=codes[:, columns].bitcast(FP8X4),
                lhsT_scale=scales[:, columns],
                rhs=moving[0],
                rhs_scale=moving[1],
                start=start,
                stop=stop,
            )

        def moved(operand):
            codes, scales = operand
            return codes[:].bitcast(FP8X4), scales[:]

        def columns_of(t):
            return slice(P * t, P * (t + 1))

        def copy(engine, out, in_):
            if engine == "s":
                nc.scalar.copy(out=out, in_=in_)
            else:
                nc.vector.tensor_copy(out=out, in_=in_)

        identity = kept([P, P], F32, "identity")
        make_identity(nc, identity[:])
        identity_bf = kept([P, P], BF16, "identity_bf")
        nc.gpsimd.tensor_copy(out=identity_bf[:], in_=identity[:])
        d_scales_sb = kept([P, CHUNKS, READOUTS], U8, "d_scales_sb")
        nc.gpsimd.memset(d_scales_sb[:].rearrange("p c n -> p (c n)").bitcast(I32), 0)

        scale_spread = kept([P, SPREAD], F32, "scale_spread")
        amp_spread = kept([P, SPREAD], BF16, "amp_spread")
        x_sb = [kept([P, 2, 2, CHANNELS], U8, "x_sb%d" % h) for h in range(HALVES)]
        enc_sb = [[kept([P, SLOTS, PASS], BF16, "enc_sb%d%d" % (g, c)) for c in range(CHUNKS)] for g in range(DEPTHS)]
        bias_sb = kept([P, CHUNKS, TILES], BF16, "bias_sb")
        amp_y = kept([P, HALVES, 2, 2], BF16, "amp_y")
        amp_attr = kept([P, HALVES, SLOTS], BF16, "amp_attr")
        d_sb = kept([P, CHUNKS, 2 * READOUTS], U8, "d_sb")
        attr_sb = [kept([P, SLOTS, ATTRIBUTES], BF16, "attr_sb%d" % h) for h in range(HALVES)]

        x_rows = x_bytes.rearrange("(h s p e) k -> h p s (e k)", h=HALVES, s=2, e=2)
        enc_rows = enc.rearrange("(g p j) f -> g p j f", p=P, j=SLOTS)
        attr_rows = attr.rearrange("(h p v) r -> h p v r", p=P, v=SLOTS)

        def load_enc(g, c):
            nc.sync.dma_start(out=enc_sb[g][c][:], in_=enc_rows[g][:, :, c * PASS : (c + 1) * PASS])

        nc.sync.dma_start(out=scale_spread[:], in_=x_scale.rearrange("o (p c) -> p (o c)", c=SPREAD))
        nc.sync.dma_start(out=amp_spread[:], in_=amp.rearrange("(p c) -> p c", c=SPREAD))
        nc.sync.dma_start(out=x_sb[0][:, 0].rearrange("p e k -> p (e k)"), in_=x_rows[0][:, 0])
        load_enc(0, 0)
        nc.sync.dma_start(out=x_sb[0][:, 1].rearrange("p e k -> p (e k)"), in_=x_rows[0][:, 1])
        load_enc(1, 0)
        load_enc(0, 1)
        load_enc(1, 1)
        nc.sync.dma_start(out=x_sb[1][:].rearrange("p s e k -> p s (e k)"), in_=x_rows[1])
        nc.sync.dma_start(out=bias_sb[:], in_=bias.rearrange("(c p t) -> p c t", p=P, t=TILES))
        load_enc(0, 2)
        load_enc(1, 2)
        nc.sync.dma_start(out=amp_y[:], in_=amp.rearrange("(h s p e) -> p h s e", h=HALVES, s=2, e=2))
        nc.sync.dma_start(out=amp_attr[:], in_=amp.rearrange("(h p v) -> p h v", p=P, v=SLOTS))
        nc.sync.dma_start(out=d_sb[:], in_=d_words.rearrange("c p n -> p c n"))
        for quadrant in range(4):
            nc.sync.dma_start(
                out=d_scales_sb[32 * quadrant : 32 * quadrant + 4, :, :].bitcast(I32),
                in_=d_scales[:, 4 * quadrant : 4 * quadrant + 4, :].rearrange("c q n -> q c n").bitcast(I32),
            )
        for h in range(HALVES):
            nc.sync.dma_start(out=attr_sb[h][:], in_=attr_rows[h])

        x_mx = [[mx_operand("x%d%d" % (h, g)) for g in range(DEPTHS)] for h in range(HALVES)]
        enc_mx = [[mx_operand("enc%d%d" % (g, c)) for c in range(CHUNKS)] for g in range(DEPTHS)]
        attr_mx = [mx_operand("attr%d" % h) for h in range(HALVES)]
        hy_mx = [[mx_operand("hy%d%d" % (h, c)) for c in range(CHUNKS)] for h in range(HALVES)]
        hz_mx = [[mx_operand("hz%d%d" % (h, c)) for c in range(CHUNKS)] for h in range(HALVES)]
        scale_sb = kept([P, CHANNELS], F32, "scale_sb")
        amp_abs = kept([P, SAMPLES], BF16, "amp_abs")
        sign_y = kept([P, HALVES * TILES], F32, "sign_y")
        sign_attr = kept([P, HALVES, SLOTS], F32, "sign_attr")

        widened, x_turned, x_grouped, enc_grouped = {}, {}, {}, {}
        attr_signed, attr_grouped = {}, {}
        pre, h_signed, h_sb, hy_grouped, hz_turned, hz_grouped = {}, {}, {}, {}, {}, {}
        y_sums, z_sums = {}, {}

        def made(table, key, shape, name, bufs):
            if key not in table:
                table[key] = staged(shape, BF16, name, bufs)
            return table[key]

        zeros = kept([P, PASS], BF16, "zeros")
        nc.vector.memset(zeros[:], 0.0)
        unread = product_bank()

        def keep_awake(*moving):
            for rhs in moving:
                nc.tensor.matmul(unread[:], lhsT=identity_bf[:], rhs=rhs, start=True, stop=True)

        def first_columns(g, c):
            return enc_grouped[g, c][:, :P, :].rearrange("p n j -> p (n j)")

        def spread_scale():
            for bank, engine in enumerate("sv"):
                rows = transpose_bank([P, 4, P])
                for c in range(4):
                    column = scale_spread[:, 4 * bank + c : 4 * bank + c + 1]
                    nc.tensor.transpose(rows[:, c, :], column.to_broadcast([P, P]), identity[:])
                by_c = scale_sb[:].rearrange("p (i c) -> p i c", c=SPREAD)
                copy(engine, by_c[:, :, 4 * bank : 4 * bank + 4], rows[:].rearrange("p c i -> p i c"))

        def spread_amp():
            rows = transpose_bank([P, SPREAD, P], BF16)
            for c in range(SPREAD):
                nc.tensor.transpose(rows[:, c, :], amp_spread[:, c : c + 1].to_broadcast([P, P]), identity_bf[:])
            for h in range(HALVES):
                nc.scalar.activation(
                    out=amp_abs[:, PASS * h : PASS * (h + 1)].rearrange("p (e i m) -> p e i m", e=2, m=4),
                    in_=rows[:, :, 64 * h : 64 * (h + 1)].rearrange("p (m e) i -> p e i m", e=2),
                    func=ACT.Abs,
                )

        def take_signs():
            nc.scalar.activation(out=sign_attr[:], in_=amp_attr[:], func=ACT.Sign)
            nc.scalar.activation(
                out=sign_y[:].rearrange("p (h e s) -> p h e s", h=HALVES, e=2),
                in_=amp_y[:].rearrange("p h s e -> p h e s"),
                func=ACT.Sign,
            )

        def widen_x(*tiles):
            for i in tiles:
                h, e, s = i // 4, i % 4 // 2, i % 2
                widened[i] = staged([P, CHANNELS], BF16, "widened", 3)
                nc.vector.tensor_tensor(
                    out=widened[i][:], in0=x_sb[h][:, s, e, :].bitcast(FP8), in1=scale_sb[:], op=ALU.mult
                )

        def turn_x(i):
            words = widened[i][:].bitcast(F32)
            x_turned[i] = transpose_bank([P, DEPTHS, 2, P])
            for g in range(DEPTHS):
                for u in range(2):
                    nc.tensor.transpose(
                        x_turned[i][:, g, u, :], words[:, 256 * g + u : 256 * (g + 1) : 2], identity[:]
                    )

        def empty_x(i, engine):
            h, tile = i // 4, i % 4
            grouped = made(x_grouped, h, [P, DEPTHS, PASS, SLOTS], "x_grouped", 1)
            words = grouped[:].rearrange("p g n j -> p (g n j)").bitcast(F32)
            words = words.rearrange("p (g n u) -> p g n u", g=DEPTHS, u=2)
            copy(engine, words[:, :, columns_of(tile), :], x_turned[i][:].rearrange("p g u n -> p g n u"))

        def quantize_x(h, *depths):
            for g in depths:
                quantize(x_mx[h][g], x_grouped[h][:, g, :, :])

        def group_enc(g, c, engine, *pieces):
            grouped = made(enc_grouped, (g, c), [P, PASS, SLOTS], "enc_grouped", 4)
            dst = grouped[:].rearrange("p (t a b) j -> p a j b t", t=TILES, b=2)
            src = enc_sb[g][c][:].rearrange("p j (a b t) -> p a j b t", b=2, t=TILES)
            for piece in pieces:
                a = slice(16 * piece, 16 * (piece + 1))
                copy(engine, dst[:, a], src[:, a])

        def quantize_enc(g, c):
            quantize(enc_mx[g][c], enc_grouped[g, c])

        def sign_rows(h, *rows):
            signed = made(attr_signed, h, [P, SLOTS, ATTRIBUTES], "attr_signed", 2)
            for v in rows:
                nc.vector.tensor_scalar_mul(signed[:, v, :], attr_sb[h][:, v, :], sign_attr[:, h, v : v + 1])

        def group_attr(h, engine, *pieces):
            grouped = made(attr_grouped, h, [P, ATTRIBUTES, SLOTS], "attr_grouped", 1)
            for piece in pieces:
                n = columns_of(piece)
                copy(
                    engine,
                    grouped[:, n, :].rearrange("p (c i) (u e) -> p c e u i", i=4, u=2),
                    attr_signed[h][:, :, n].rearrange("p (e u) (c i) -> p c e u i", i=4, e=2),
                )

        def quantize_attr(h):
            quantize(attr_mx[h], attr_grouped[h])

        def encode(h, c, *tiles):
            for t in tiles:
                pre[h, c, t] = product_bank()
                for g in range(DEPTHS):
                    multiply(
                        pre[h, c, t][:], enc_mx[g][c], columns_of(t), moved(x_mx[h][g]), g == 0, g == DEPTHS - 1
                    )

        def scale_h(h, c, *tiles):
            signed = made(h_signed, (h, c), [P, TILES, PASS], "h_signed", 3)
            for t in tiles:
                nc.vector.scalar_tensor_tensor(
                    out=signed[:, t, :],
                    in0=pre[h, c, t][:],
                    scalar=bias_sb[:, c, t : t + 1],
                    in1=amp_abs[:, PASS * h : PASS * (h + 1)],
                    op0=ALU.add,
                    op1=ALU.mult,
                )

        def relu(h, c):
            rectified = made(h_sb, (h, c), [P, TILES, PASS], "h_sb", 3)
            nc.vector.tensor_scalar_max(rectified[:], h_signed[h, c][:], 0.0)

        def group_hy(h, c, engine, *pieces):
            grouped = made(hy_grouped, (h, c), [P, PASS, SLOTS], "hy_grouped", 3)
            for piece in pieces:
                n = columns_of(piece)
                copy(
                    engine,
                    grouped[:, n, :].rearrange("p (c i) t -> p c t i", i=4),
                    h_sb[h, c][:, :, n].rearrange("p t (c i) -> p c t i", i=4),
                )

        def quantize_hy(h, c):
            quantize(hy_mx[h][c], hy_grouped[h, c])

        def turn_hz(h, c, *pairs):
            for pair in pairs:
                hz_turned[h, c, pair] = transpose_bank([P, 2, 2, P])
                for k in range(2):
                    words = h_sb[h, c][:, 2 * pair + k, :].bitcast(F32)
                    for u in range(2):
                        nc.tensor.transpose(
                            hz_turned[h, c, pair][:, k, u, :], words[:, columns_of(u)], identity[:]
                        )

        def empty_hz(h, c, pair, engine):
            grouped = made(hz_grouped, (h, c), [P, PASS, SLOTS], "hz_grouped", 3)
            words = grouped[:].rearrange("p n j -> p (n j)").bitcast(F32)
            words = words.rearrange("p (t n u) -> p t n u", t=TILES, u=2)
            copy(
                engine,
                words[:, 2 * pair : 2 * pair + 2],
                hz_turned[h, c, pair][:].rearrange("p t u n -> p t n u"),
            )

        def quantize_hz(h, c):
            quantize(hz_mx[h][c], hz_grouped[h, c])

        y_rows = out_0.rearrange("(h s p e) c -> h e s p c", h=HALVES, s=2, e=2)

        def read_out(i, n, *chunks):
            if chunks[0] == 0:
                y_sums[i, n] = product_bank()
            for c in chunks:
                d = (
                    d_sb[:, c, 2 * PASS * n : 2 * PASS * (n + 1)].bitcast(FP4X4),
                    d_scales_sb[:, c, PASS * n : PASS * (n + 1)],
                )
                multiply(y_sums[i, n][:], hy_mx[i // 4][c], columns_of(i % 4), d, c == 0, c == CHUNKS - 1)

        def store_y(i, n, engine):
            result = work.tile([P, PASS], F32, name="y_result", bufs=8)
            sign = sign_y[:, i : i + 1]
            if engine == "s":
                nc.scalar.activation(out=result[:], in_=y_sums[i, n][:], func=ACT.Copy, scale=sign)
            else:
                nc.vector.tensor_scalar_mul(result[:], y_sums[i, n][:], sign)
            rows = y_rows[i // 4][i % 4 // 2][i % 2]
            nc.sync.dma_start(out=rows[:, PASS * n : PASS * (n + 1)], in_=result[:])

        z_rows = out_1.rearrange("(c p t) r -> c t p r", p=P, t=TILES)

        def associate(c, *tiles):
            for t in tiles:
                z_sums[c, t] = product_bank()
                for h in range(HALVES):
                    multiply(
                        z_sums[c, t][:], hz_mx[h][c], columns_of(t), moved(attr_mx[h]), h == 0, h == HALVES - 1
                    )

        def store_z(c, t, engine):
            result = work.tile([P, ATTRIBUTES], F32, name="z_result", bufs=4)
            copy(engine, result[:], z_sums[c, t][:])
            nc.sync.dma_start(out=z_rows[c][t], in_=result[:])

        spread_scale()
        spread_amp()
        keep_awake(zeros[:], zeros[:], zeros[:])
        widen_x(0)
        group_enc(0, 0, "s", 0, 2, 3)
        group_enc(0, 0, "v", 1)
        group_enc(1, 0, "s", 0)
        widen_x(2, 1)
        turn_x(0)
        keep_awake(widened[0][:, :PASS])
        turn_x(2)
        keep_awake(widened[2][:, :PASS])
        widen_x(3)
        empty_x(2, "s")
        group_enc(0, 1, "s", 0)
        quantize_enc(0, 0)
        empty_x(0, "s")
        turn_x(3)
        keep_awake(widened[3][:, :PASS])
        group_enc(1, 0, "v", 1, 2, 3)
        group_enc(1, 1, "s", 0)
        group_enc(1, 1, "v", 1)
        turn_x(1)
        keep_awake(widened[1][:, :PASS], first_columns(0, 0), first_columns(1, 0))
        empty_x(3, "s")
        empty_x(1, "s")
        quantize_enc(1, 0)
        widen_x(4)

        group_enc(1, 1, "s", 2)
        group_enc(0, 1, "s", 1)
        group_enc(1, 1, "s", 3)
        group_enc(0, 1, "s", 3)
        group_enc(0, 2, "s", 0)
        quantize_x(0, 0, 1)
        group_enc(0, 1, "v", 2)
        group_enc(1, 2, "s", 0)
        group_enc(0, 2, "s", 1, 2, 3)
        encode(0, 0, 0, 1, 2, 3)
        widen_x(5)
        quantize_enc(1, 1)
        quantize_enc(0, 1)
        scale_h(0, 0, 0, 3, 1, 2)
        encode(0, 1, 0, 1, 2, 3)
        group_enc(1, 2, "s", 1, 2, 3)
        quantize_enc(0, 2)
        relu(0, 0)
        scale_h(0, 1, 1)
        group_hy(0, 0, "s", 0, 1)
        turn_hz(0, 0, 0, 1)
        quantize_enc(1, 2)
        scale_h(0, 1, 3, 0, 2)
        encode(0, 2, 0)
        empty_hz(0, 0, 0, "s")
        empty_hz(0, 0, 1, "s")
        widen_x(6)
        take_signs()
        group_hy(0, 0, "s", 2, 3)
        turn_x(4)
        encode(0, 2, 1, 2, 3)
        relu(0, 1)
        empty_x(4, "s")
        scale_h(0, 2, 0, 2, 3)
        group_hy(0, 1, "s", 0, 1)
        group_hy(0, 1, "v", 2)
        turn_x(6)
        turn_x(5)
        empty_x(6, "s")
        quantize_hy(0, 0)
        group_hy(0, 1, "s", 3)
        scale_h(0, 2, 1)
        turn_hz(0, 1, 0)
        empty_hz(0, 1, 0, "s")
        quantize_hy(0, 1)
        empty_x(5, "s")
        relu(0, 2)

        read_out(0, 0, 0, 1)
        read_out(0, 1, 0, 1)
        read_out(1, 0, 0, 1)
        read_out(1, 1, 0, 1)
        sign_rows(0, 0, 1)
        group_hy(0, 2, "s", 0, 1, 2)
        widen_x(7)
        sign_rows(0, 2)
        group_hy(0, 2, "v", 3)
        turn_hz(0, 2, 0)
        sign_rows(0, 3)
        quantize_hz(0, 0)
        group_attr(0, "s", 0)
        turn_x(7)
        quantize_hy(0, 2)
        read_out(2, 0, 0, 1)
        read_out(2, 1, 0, 1)
        read_out(2, 1, 2)
        read_out(1, 1, 2)
        read_out(0, 0, 2)
        read_out(0, 1, 2)
        read_out(1, 0, 2)
        read_out(2, 0, 2)
        empty_x(7, "s")
        group_attr(0, "v", 1, 2)
        sign_rows(1, 0)
        store_y(2, 1, "s")
        store_y(1, 1, "s")
        store_y(1, 0, "s")
        store_y(0, 0, "s")
        quantize_x(1, 0, 1)
        sign_rows(1, 1, 2)

        encode(1, 0, 0, 1)
        group_attr(0, "v", 3)
        sign_rows(1, 3)
        scale_h(1, 0, 0, 1)
        turn_hz(0, 1, 1)
        empty_hz(0, 1, 1, "s")
        quantize_attr(0)
        encode(1, 0, 2, 3)
        encode(1, 1, 0, 1)
        store_y(0, 1, "s")
        scale_h(1, 0, 2, 3)
        scale_h(1, 1, 0)
        group_attr(1, "s", 0)
        store_y(2, 0, "s")
        empty_hz(0, 2, 0, "s")
        relu(1, 0)
        encode(1, 2, 0)
        group_attr(1, "s", 1)
        group_attr(1, "v", 2)
        turn_hz(0, 2, 1)
        group_hy(1, 0, "v", 0)
        empty_hz(0, 2, 1, "s")
        encode(1, 1, 2)
        scale_h(1, 1, 1, 2)
        group_attr(1, "s", 3)
        turn_hz(1, 0, 0, 1)
        group_hy(1, 0, "s", 1, 2)
        quantize_hz(0, 1)
        encode(1, 1, 3)
        scale_h(1, 1, 3)
        read_out(3, 0, 0, 1, 2)
        read_out(3, 1, 0, 1, 2)
        quantize_attr(1)
        empty_hz(1, 0, 0, "s")
        empty_hz(1, 0, 1, "s")
        relu(1, 1)
        quantize_hz(0, 2)
        group_hy(1, 0, "s", 3)
        encode(1, 2, 1, 2)
        scale_h(1, 2, 0, 1)
        store_y(3, 1, "s")
        store_y(3, 0, "s")
        turn_hz(1, 1, 0, 1)
        quantize_hz(1, 0)
        empty_hz(1, 1, 1, "s")
        empty_hz(1, 1, 0, "s")
        encode(1, 2, 3)
        scale_h(1, 2, 2, 3)

        associate(0, 0, 1, 2)
        group_hy(1, 1, "s", 0)
        quantize_hz(1, 1)
        store_z(0, 0, "s")
        store_z(0, 1, "s")
        store_z(0, 2, "s")
        relu(1, 2)
        associate(1, 0)
        associate(0, 3)
        associate(1, 1)
        group_hy(1, 1, "v", 1)
        group_hy(1, 2, "v", 0)
        group_hy(1, 1, "v", 2)
        group_hy(1, 1, "s", 3)
        group_hy(1, 2, "v", 1)
        group_hy(1, 2, "s", 2, 3)
        quantize_hy(1, 0)
        turn_hz(1, 2, 0, 1)
        store_z(0, 3, "v")
        store_z(1, 0, "s")
        associate(1, 2, 3)
        quantize_hy(1, 1)
        quantize_hy(1, 2)
        store_z(1, 3, "s")
        empty_hz(1, 2, 0, "v")

        read_out(4, 0, 0, 1, 2)
        read_out(4, 1, 0, 1, 2)
        read_out(5, 0, 0, 1, 2)
        read_out(5, 1, 0, 1, 2)
        store_z(1, 1, "v")
        store_y(4, 0, "s")
        empty_hz(1, 2, 1, "s")
        store_z(1, 2, "v")
        store_y(4, 1, "v")
        store_y(5, 0, "v")
        store_y(5, 1, "s")
        read_out(6, 0, 0, 1, 2)
        read_out(6, 1, 0, 1, 2)
        read_out(7, 0, 0, 1, 2)
        read_out(7, 1, 0, 1, 2)
        store_y(6, 0, "v")
        store_y(6, 1, "s")
        store_y(7, 0, "s")
        store_y(7, 1, "s")
        quantize_hz(1, 2)
        associate(2, 0, 1, 2, 3)
        store_z(2, 0, "v")
        store_z(2, 1, "v")
        store_z(2, 2, "v")
        store_z(2, 3, "s")
